import numpy as np
CORES = [24,25,26,27,48,49,50,51,72,73,74,75,96,97,98,99]
N = 16
TK, LAY = 512, 4
def setup_inputs(rng):
    return {"x": rng.standard_normal((N, 128, TK), dtype=np.float32), "w": (rng.standard_normal((N, 128, LAY * 256), dtype=np.float32) / 16)}
def setup_inputs_big(rng):
    d = setup_inputs(rng)
    for k in ("x",): d[k] = (d[k].astype(np.float32) * 1048576.0).astype(d[k].dtype)
    return d
def setup_inputs_small(rng):
    d = setup_inputs(rng)
    for k in ("x",): d[k] = (d[k].astype(np.float32) * (1 / 1048576.0)).astype(d[k].dtype)
    return d
def setup_inputs_apart(rng):
    d = setup_inputs(rng)
    f = (10.0 ** rng.permutation(np.linspace(-1.5, 1.5, N))).astype(np.float32).reshape(N, 1, 1)
    for k in ("x",): d[k] = (d[k].astype(np.float32) * f).astype(d[k].dtype)
    return d
def reference(x, w):
    X, W = x.astype(np.float64), w.astype(np.float64)
    h = list(X)
    for l in range(LAY):
        h = [np.maximum(W[r][:, 256 * l:256 * l + 128].T @ h[r] + W[r][:, 256 * l + 128:256 * l + 256].T @ h[r ^ (1 << l)], 0.0) for r in range(N)]
    return {"y": np.stack(h).astype(np.float32)}

@@ -1,0 +1,176 @@
+from concourse.bass import DstId, RemoteDMATransfer
+from concourse.mybir import AluOpType
+
+N, LAY, TK = 16, 4, 512
+SIM_CORES = 112
+WIDTHS = [256, 256]
+C = len(WIDTHS)
+WMAX = max(WIDTHS)
+BANKS = 8
+
+SCRATCH = {"ws": ("sbuf", [128, LAY * 256], "float32"), "zero": ("sbuf", [128, WMAX], "float32")}
+for _l in range(LAY + 1):
+    SCRATCH["hs%d" % _l] = ("sbuf", [128, TK], "float32")
+for _l in range(LAY):
+    SCRATCH["hp%d" % _l] = ("sbuf", [128, TK], "float32")
+for _b in range(BANKS):
+    SCRATCH["ps%d" % _b] = ("psum", [128, 512], "float32")
+
+SEMAPHORES = ["zs", "snt", "aw", "lw0", "lw1", "lw2"]
+SEMAPHORES += ["lx%d" % c for c in range(C)] + ["st%d" % c for c in range(C)]
+for _k in ("as", "ap", "mm", "rl"):
+    SEMAPHORES += ["%s%d_%d" % (_k, l, c) for l in range(LAY) for c in range(C)]
+
+
+def _bits(m):
+    return [b for b in range(m.bit_length()) if (m >> b) & 1]
+
+
+def _plan(T, topo):
+    home = list(T.cores)
+    hard = [l for l in range(LAY) if not all(topo.may_write(home[r], home[r ^ (1 << l)]) for r in range(N))]
+    lo, hi = min(hard) - 1, max(hard) + 1
+    taken = set(home)
+    stand = []
+    for r in range(N):
+        far = [home[r ^ (1 << l)] for l in hard]
+        if all(topo.may_write(home[r], f) for f in far):
+            stand.append(home[r])
+            continue
+        free = [c for c in range(SIM_CORES) if c not in taken and topo.chip(c) == topo.chip(home[r])
+                and all(topo.may_write(c, f) for f in far)]
+        free.sort(key=lambda c: (topo.die(c) == topo.die(home[r]), c))
+        stand.append(free[0])
+        taken.add(free[0])
+    place = [stand if lo <= l < hi else home for l in range(LAY)]
+    return home, place, lo, hi
+
+
+def rank_program(g, core, T, topo):
+    home, place, lo, hi = _plan(T, topo)
+    mine = {l: r for l in range(LAY) for r in range(N) if place[l][r] == core}
+    if not mine:
+        return
+    rank = T.rank_of(core)
+    sem = T.sem
+    cols = [slice(sum(WIDTHS[:c]), sum(WIDTHS[:c + 1])) for c in range(C)]
+    pieces = [(0, lo), (lo, hi), (hi, LAY)]
+
+    def src(l, r):
+        return home[r] if l == 0 else place[l - 1][r]
+
+    def routes(l, r):
+        s = src(l, r)
+        out = [(place[l][r], "s")] if place[l][r] != s else []
+        out.append((place[l][r ^ (1 << l)], "p"))
+        m = [topo.mask(s, d) for d, _ in out]
+        if len(m) == 2:
+            if m[0] == m[1]:
+                b = _bits(m[0])
+                m = [sum(1 << x for x in b[:len(b) // 2]), sum(1 << x for x in b[len(b) // 2:])]
+            elif len(_bits(m[0])) < len(_bits(m[1])):
+                m[1] &= ~m[0]
+            else:
+                m[0] &= ~m[1]
+        return [(d, k, mm) for (d, k), mm in zip(out, m)]
+
+    def landed(l, r, kind):
+        who = r if kind == "s" else r ^ (1 << l)
+        return [len(_bits(m)) for d, k, m in routes(l, who) if k == kind][0]
+
+    dq = [g.sync, g.scalar]
+    if rank is not None:
+        for c in range(C):
+            dq[c % 2].dma_start(T.hs0[:, cols[c]], T.x[:, cols[c]]).then_inc(sem["lx%d" % c], 16)
+        for i, q in ((0, g.sync), (1, g.scalar), (2, g.sync)):
+            a, b = pieces[i]
+            q.dma_start(T.ws[:, 256 * a:256 * b], T.w[:, 256 * a:256 * b]).then_inc(sem["lw%d" % i], 16)
+
+    sent = [0]
+
+    def send(l, r, c):
+        buf = T["hs%d" % l]
+        tr = []
+        for d, k, m in routes(l, r):
+            rid, pid, _ = topo.addr(d)
+            dst = T["h%s%d" % (k, l)]
+            tr.append((rid, pid, m, dst[:, cols[c]], sem["a%s%d_%d" % (k, l, c)]))
+            sent[0] += len(_bits(m))
+        if len(tr) == 1:
+            rid, pid, m, dst, rs = tr[0]
+            g.remote_dma(out_ap=dst, in_ap=buf[:, cols[c]], remote_sem=rs, local_sem=sem.snt, pid=pid, routing_id=rid,
+                         dma_engine_mask=m)
+        else:
+            g.remote_dma_fused([RemoteDMATransfer(dst_ids=[DstId(rid=rid, pnc=pid)], dma_engine_mask=m, remote_sem=rs,
+                                                  src=buf[:, cols[c]], dst=dst) for rid, pid, m, dst, rs in tr],
+                               local_sem=sem.snt)
+
+    if rank is not None:
+        for c in range(C):
+            g.wait_ge(sem["lx%d" % c], 16)
+            send(0, rank, c)
+        if place[lo][rank] != core:
+            d = place[lo][rank]
+            rid, pid, _ = topo.addr(d)
+            g.wait_ge(sem.lw1, 16)
+            g.remote_dma(out_ap=T.ws[:, 256 * lo:256 * hi], in_ap=T.ws[:, 256 * lo:256 * hi], remote_sem=sem.aw,
+                         local_sem=sem.snt, pid=pid, routing_id=rid, dma_engine_mask=topo.mask(core, d))
+            sent[0] += len(_bits(topo.mask(core, d)))
+    for l in range(1, LAY):
+        if l - 1 in mine:
+            for c in range(C):
+                g.wait_ge(sem["rl%d_%d" % (l - 1, c)], 1)
+                send(l, mine[l - 1], c)
+
+    bank = {}
+    reader = {}
+    nb = 0
+    for l in sorted(mine):
+        r = mine[l]
+        if core == home[r]:
+            i = [j for j, (a, b) in enumerate(pieces) if a <= l < b][0]
+            g.tensor.wait_ge(sem["lw%d" % i], 16)
+        else:
+            g.tensor.wait_ge(sem.aw, len(_bits(topo.mask(home[r], core))))
+        wt = {"s": T.ws[:, 256 * l:256 * l + 128], "p": T.ws[:, 256 * l + 128:256 * l + 256]}
+        s_src, p_src = src(l, r), src(l, r ^ (1 << l))
+        if s_src != core and topo.chip(s_src) == topo.chip(p_src):
+            order = [(k, c) for c in range(C) for k in ("p", "s")]
+        else:
+            order = [("s", c) for c in range(C)] + [("p", c) for c in range(C)]
+        for k, c in order:
+            first = (l, c) not in bank
+            if first:
+                bank[(l, c)] = nb % BANKS
+                if bank[(l, c)] in reader:
+                    g.tensor.wait_ge(reader[bank[(l, c)]], 1)
+                reader[bank[(l, c)]] = sem["rl%d_%d" % (l, c)]
+                nb += 1
+            if k == "p" or s_src != core:
+                g.tensor.wait_ge(sem["a%s%d_%d" % (k, l, c)], landed(l, r, k))
+            elif l == 0:
+                g.tensor.wait_ge(sem["lx%d" % c], 16)
+            else:
+                g.tensor.wait_ge(sem["rl%d_%d" % (l - 1, c)], 1)
+            mm = g.tensor.matmul(T["ps%d" % bank[(l, c)]][:, 0:WIDTHS[c]], wt[k], T["h%s%d" % (k, l)][:, cols[c]],
+                                 first, not first)
+            if not first:
+                mm.then_inc(sem["mm%d_%d" % (l, c)], 1)
+
+    g.vector.memset(T.zero[:], 0.0).then_inc(sem.zs, 1)
+    g.vector.wait_ge(sem.zs, 1)
+    for l in sorted(mine):
+        for c in range(C):
+            g.vector.wait_ge(sem["mm%d_%d" % (l, c)], 1)
+            g.vector.tensor_tensor(T["hs%d" % (l + 1)][:, cols[c]], T["ps%d" % bank[(l, c)]][:, 0:WIDTHS[c]],
+                                   T.zero[:, 0:WIDTHS[c]], AluOpType.max).then_inc(sem["rl%d_%d" % (l, c)], 1)
+
+    if LAY - 1 in mine:
+        for c in range(C):
+            q = dq[c % 2]
+            q.wait_ge(sem["rl%d_%d" % (LAY - 1, c)], 1)
+            q.dma_start(T.y[:, cols[c]], T["hs%d" % LAY][:, cols[c]]).then_inc(sem["st%d" % c], 16)
+    g.wait_ge(sem.snt, sent[0])
+    if LAY - 1 in mine:
+        for c in range(C):
+            g.wait_ge(sem["st%d" % c], 16)

@@ -3,7 +3,7 @@ from concourse.mybir import AluOpType
 
 N, LAY, TK = 16, 4, 512
 SIM_CORES = 112
-WIDTHS = [256, 256]
+WIDTHS = [176, 176, 160]
 C = len(WIDTHS)
 WMAX = max(WIDTHS)
 BANKS = 8

@@ -3,7 +3,7 @@ from concourse.mybir import AluOpType
 
 N, LAY, TK = 16, 4, 512
 SIM_CORES = 112
-WIDTHS = [176, 176, 160]
+WIDTHS = [128, 128, 128, 128]
 C = len(WIDTHS)
 WMAX = max(WIDTHS)
 BANKS = 8
@@ -16,7 +16,7 @@ for _l in range(LAY):
 for _b in range(BANKS):
     SCRATCH["ps%d" % _b] = ("psum", [128, 512], "float32")
 
-SEMAPHORES = ["zs", "snt", "aw", "lw0", "lw1", "lw2"]
+SEMAPHORES = ["zs", "snt", "aw", "lu", "lv", "lw1", "lw2"]
 SEMAPHORES += ["lx%d" % c for c in range(C)] + ["st%d" % c for c in range(C)]
 for _k in ("as", "ap", "mm", "rl"):
     SEMAPHORES += ["%s%d_%d" % (_k, l, c) for l in range(LAY) for c in range(C)]
@@ -66,8 +66,7 @@ def rank_program(g, core, T, topo):
         m = [topo.mask(s, d) for d, _ in out]
         if len(m) == 2:
             if m[0] == m[1]:
-                b = _bits(m[0])
-                m = [sum(1 << x for x in b[:len(b) // 2]), sum(1 << x for x in b[len(b) // 2:])]
+                out.reverse()
             elif len(_bits(m[0])) < len(_bits(m[1])):
                 m[1] &= ~m[0]
             else:
@@ -80,9 +79,11 @@ def rank_program(g, core, T, topo):
 
     dq = [g.sync, g.scalar]
     if rank is not None:
+        g.scalar.dma_start(T.ws[:, 0:128], T.w[:, 0:128]).then_inc(sem.lu, 16)
         for c in range(C):
             dq[c % 2].dma_start(T.hs0[:, cols[c]], T.x[:, cols[c]]).then_inc(sem["lx%d" % c], 16)
-        for i, q in ((0, g.sync), (1, g.scalar), (2, g.sync)):
+        g.sync.dma_start(T.ws[:, 128:256 * lo], T.w[:, 128:256 * lo]).then_inc(sem.lv, 16)
+        for i, q in ((1, g.scalar), (2, g.sync)):
             a, b = pieces[i]
             q.dma_start(T.ws[:, 256 * a:256 * b], T.w[:, 256 * a:256 * b]).then_inc(sem["lw%d" % i], 16)
 
@@ -96,10 +97,10 @@ def rank_program(g, core, T, topo):
             dst = T["h%s%d" % (k, l)]
             tr.append((rid, pid, m, dst[:, cols[c]], sem["a%s%d_%d" % (k, l, c)]))
             sent[0] += len(_bits(m))
-        if len(tr) == 1:
-            rid, pid, m, dst, rs = tr[0]
-            g.remote_dma(out_ap=dst, in_ap=buf[:, cols[c]], remote_sem=rs, local_sem=sem.snt, pid=pid, routing_id=rid,
-                         dma_engine_mask=m)
+        if len(tr) == 1 or tr[0][2] & tr[1][2]:
+            for rid, pid, m, dst, rs in tr:
+                g.remote_dma(out_ap=dst, in_ap=buf[:, cols[c]], remote_sem=rs, local_sem=sem.snt, pid=pid,
+                             routing_id=rid, dma_engine_mask=m)
         else:
             g.remote_dma_fused([RemoteDMATransfer(dst_ids=[DstId(rid=rid, pnc=pid)], dma_engine_mask=m, remote_sem=rs,
                                                   src=buf[:, cols[c]], dst=dst) for rid, pid, m, dst, rs in tr],
@@ -125,17 +126,20 @@ def rank_program(g, core, T, topo):
     bank = {}
     reader = {}
     nb = 0
+    seen_v = []
     for l in sorted(mine):
         r = mine[l]
         if core == home[r]:
             i = [j for j, (a, b) in enumerate(pieces) if a <= l < b][0]
-            g.tensor.wait_ge(sem["lw%d" % i], 16)
+            g.tensor.wait_ge(sem["lw%d" % i] if i else sem.lu, 16)
         else:
             g.tensor.wait_ge(sem.aw, len(_bits(topo.mask(home[r], core))))
         wt = {"s": T.ws[:, 256 * l:256 * l + 128], "p": T.ws[:, 256 * l + 128:256 * l + 256]}
         s_src, p_src = src(l, r), src(l, r ^ (1 << l))
         if s_src != core and topo.chip(s_src) == topo.chip(p_src):
             order = [(k, c) for c in range(C) for k in ("p", "s")]
+        elif s_src != core:
+            order = [(k, c) for c in range(C) for k in ("s", "p")]
         else:
             order = [("s", c) for c in range(C)] + [("p", c) for c in range(C)]
         for k, c in order:
@@ -146,6 +150,9 @@ def rank_program(g, core, T, topo):
                     g.tensor.wait_ge(reader[bank[(l, c)]], 1)
                 reader[bank[(l, c)]] = sem["rl%d_%d" % (l, c)]
                 nb += 1
+            if k == "p" and l < lo and not seen_v:
+                g.tensor.wait_ge(sem.lv, 16)
+                seen_v.append(1)
             if k == "p" or s_src != core:
                 g.tensor.wait_ge(sem["a%s%d_%d" % (k, l, c)], landed(l, r, k))
             elif l == 0:

from concourse.bass import DstId, RemoteDMATransfer
from concourse.mybir import AluOpType

N, LAY, TK = 16, 4, 512
SIM_CORES = 112
WIDTHS = [128, 128, 128, 128]
C = len(WIDTHS)
WMAX = max(WIDTHS)
BANKS = 8

SCRATCH = {"ws": ("sbuf", [128, LAY * 256], "float32"), "zero": ("sbuf", [128, WMAX], "float32")}
for _l in range(LAY + 1):
    SCRATCH["hs%d" % _l] = ("sbuf", [128, TK], "float32")
for _l in range(LAY):
    SCRATCH["hp%d" % _l] = ("sbuf", [128, TK], "float32")
for _b in range(BANKS):
    SCRATCH["ps%d" % _b] = ("psum", [128, 512], "float32")

SEMAPHORES = ["zs", "snt", "aw", "lu", "lv", "lw1", "lw2"]
SEMAPHORES += ["lx%d" % c for c in range(C)] + ["st%d" % c for c in range(C)]
for _k in ("as", "ap", "mm", "rl"):
    SEMAPHORES += ["%s%d_%d" % (_k, l, c) for l in range(LAY) for c in range(C)]


def _bits(m):
    return [b for b in range(m.bit_length()) if (m >> b) & 1]


def _plan(T, topo):
    home = list(T.cores)
    hard = [l for l in range(LAY) if not all(topo.may_write(home[r], home[r ^ (1 << l)]) for r in range(N))]
    lo, hi = min(hard) - 1, max(hard) + 1
    taken = set(home)
    stand = []
    for r in range(N):
        far = [home[r ^ (1 << l)] for l in hard]
        if all(topo.may_write(home[r], f) for f in far):
            stand.append(home[r])
            continue
        free = [c for c in range(SIM_CORES) if c not in taken and topo.chip(c) == topo.chip(home[r])
                and all(topo.may_write(c, f) for f in far)]
        free.sort(key=lambda c: (topo.die(c) == topo.die(home[r]), c))
        stand.append(free[0])
        taken.add(free[0])
    place = [stand if lo <= l < hi else home for l in range(LAY)]
    return home, place, lo, hi


def rank_program(g, core, T, topo):
    home, place, lo, hi = _plan(T, topo)
    mine = {l: r for l in range(LAY) for r in range(N) if place[l][r] == core}
    if not mine:
        return
    rank = T.rank_of(core)
    sem = T.sem
    cols = [slice(sum(WIDTHS[:c]), sum(WIDTHS[:c + 1])) for c in range(C)]
    pieces = [(0, lo), (lo, hi), (hi, LAY)]

    def src(l, r):
        return home[r] if l == 0 else place[l - 1][r]

    def routes(l, r):
        s = src(l, r)
        out = [(place[l][r], "s")] if place[l][r] != s else []
        out.append((place[l][r ^ (1 << l)], "p"))
        m = [topo.mask(s, d) for d, _ in out]
        if len(m) == 2:
            if m[0] == m[1]:
                out.reverse()
            elif len(_bits(m[0])) < len(_bits(m[1])):
                m[1] &= ~m[0]
            else:
                m[0] &= ~m[1]
        return [(d, k, mm) for (d, k), mm in zip(out, m)]

    def landed(l, r, kind):
        who = r if kind == "s" else r ^ (1 << l)
        return [len(_bits(m)) for d, k, m in routes(l, who) if k == kind][0]

    dq = [g.sync, g.scalar]
    if rank is not None:
        g.scalar.dma_start(T.ws[:, 0:128], T.w[:, 0:128]).then_inc(sem.lu, 16)
        for c in range(C):
            dq[c % 2].dma_start(T.hs0[:, cols[c]], T.x[:, cols[c]]).then_inc(sem["lx%d" % c], 16)
        g.sync.dma_start(T.ws[:, 128:256 * lo], T.w[:, 128:256 * lo]).then_inc(sem.lv, 16)
        for i, q in ((1, g.scalar), (2, g.sync)):
            a, b = pieces[i]
            q.dma_start(T.ws[:, 256 * a:256 * b], T.w[:, 256 * a:256 * b]).then_inc(sem["lw%d" % i], 16)

    sent = [0]

    def send(l, r, c):
        buf = T["hs%d" % l]
        tr = []
        for d, k, m in routes(l, r):
            rid, pid, _ = topo.addr(d)
            dst = T["h%s%d" % (k, l)]
            tr.append((rid, pid, m, dst[:, cols[c]], sem["a%s%d_%d" % (k, l, c)]))
            sent[0] += len(_bits(m))
        if len(tr) == 1 or tr[0][2] & tr[1][2]:
            for rid, pid, m, dst, rs in tr:
                g.remote_dma(out_ap=dst, in_ap=buf[:, cols[c]], remote_sem=rs, local_sem=sem.snt, pid=pid,
                             routing_id=rid, dma_engine_mask=m)
        else:
            g.remote_dma_fused([RemoteDMATransfer(dst_ids=[DstId(rid=rid, pnc=pid)], dma_engine_mask=m, remote_sem=rs,
                                                  src=buf[:, cols[c]], dst=dst) for rid, pid, m, dst, rs in tr],
                               local_sem=sem.snt)

    if rank is not None:
        for c in range(C):
            g.wait_ge(sem["lx%d" % c], 16)
            send(0, rank, c)
        if place[lo][rank] != core:
            d = place[lo][rank]
            rid, pid, _ = topo.addr(d)
            g.wait_ge(sem.lw1, 16)
            g.remote_dma(out_ap=T.ws[:, 256 * lo:256 * hi], in_ap=T.ws[:, 256 * lo:256 * hi], remote_sem=sem.aw,
                         local_sem=sem.snt, pid=pid, routing_id=rid, dma_engine_mask=topo.mask(core, d))
            sent[0] += len(_bits(topo.mask(core, d)))
    for l in range(1, LAY):
        if l - 1 in mine:
            for c in range(C):
                g.wait_ge(sem["rl%d_%d" % (l - 1, c)], 1)
                send(l, mine[l - 1], c)

    bank = {}
    reader = {}
    nb = 0
    seen_v = []
    for l in sorted(mine):
        r = mine[l]
        if core == home[r]:
            i = [j for j, (a, b) in enumerate(pieces) if a <= l < b][0]
            g.tensor.wait_ge(sem["lw%d" % i] if i else sem.lu, 16)
        else:
            g.tensor.wait_ge(sem.aw, len(_bits(topo.mask(home[r], core))))
        wt = {"s": T.ws[:, 256 * l:256 * l + 128], "p": T.ws[:, 256 * l + 128:256 * l + 256]}
        s_src, p_src = src(l, r), src(l, r ^ (1 << l))
        if s_src != core and topo.chip(s_src) == topo.chip(p_src):
            order = [(k, c) for c in range(C) for k in ("p", "s")]
        elif s_src != core:
            order = [(k, c) for c in range(C) for k in ("s", "p")]
        else:
            order = [("s", c) for c in range(C)] + [("p", c) for c in range(C)]
        for k, c in order:
            first = (l, c) not in bank
            if first:
                bank[(l, c)] = nb % BANKS
                if bank[(l, c)] in reader:
                    g.tensor.wait_ge(reader[bank[(l, c)]], 1)
                reader[bank[(l, c)]] = sem["rl%d_%d" % (l, c)]
                nb += 1
            if k == "p" and l < lo and not seen_v:
                g.tensor.wait_ge(sem.lv, 16)
                seen_v.append(1)
            if k == "p" or s_src != core:
                g.tensor.wait_ge(sem["a%s%d_%d" % (k, l, c)], landed(l, r, k))
            elif l == 0:
                g.tensor.wait_ge(sem["lx%d" % c], 16)
            else:
                g.tensor.wait_ge(sem["rl%d_%d" % (l - 1, c)], 1)
            mm = g.tensor.matmul(T["ps%d" % bank[(l, c)]][:, 0:WIDTHS[c]], wt[k], T["h%s%d" % (k, l)][:, cols[c]],
                                 first, not first)
            if not first:
                mm.then_inc(sem["mm%d_%d" % (l, c)], 1)

    g.vector.memset(T.zero[:], 0.0).then_inc(sem.zs, 1)
    g.vector.wait_ge(sem.zs, 1)
    for l in sorted(mine):
        for c in range(C):
            g.vector.wait_ge(sem["mm%d_%d" % (l, c)], 1)
            g.vector.tensor_tensor(T["hs%d" % (l + 1)][:, cols[c]], T["ps%d" % bank[(l, c)]][:, 0:WIDTHS[c]],
                                   T.zero[:, 0:WIDTHS[c]], AluOpType.max).then_inc(sem["rl%d_%d" % (l, c)], 1)

    if LAY - 1 in mine:
        for c in range(C):
            q = dq[c % 2]
            q.wait_ge(sem["rl%d_%d" % (LAY - 1, c)], 1)
            q.dma_start(T.y[:, cols[c]], T["hs%d" % LAY][:, cols[c]]).then_inc(sem["st%d" % c], 16)
    g.wait_ge(sem.snt, sent[0])
    if LAY - 1 in mine:
        for c in range(C):
            g.wait_ge(sem["st%d" % c], 16)
